import numpy as np, ml_dtypes
CORES = [0,1]
N = 2
def setup_inputs(rng):
    return {"x": rng.standard_normal((N, 128, 1), dtype=np.float32).astype(ml_dtypes.bfloat16)}
def reference(x):
    s = x.sum(axis=0, dtype=np.float64).astype(x.dtype)
    return {"y": np.broadcast_to(s, (N,) + s.shape)}

@@ -1,0 +1,30 @@
+from concourse.mybir import AluOpType
+
+SCRATCH = {
+    "mine": ("sbuf", [128, 1], "bfloat16"),
+    "land": ("sbuf", [128, 1], "bfloat16"),
+}
+SEMAPHORES = ["loaded", "seeded", "sent", "arrived", "stored"]
+
+ONE_ENGINE = 0x1
+
+
+def rank_program(g, core, T, topo):
+    rank = T.rank_of(core)
+    if rank is None:
+        return
+    peer = T.cores[1 - rank]
+    rid, pid, _sengine = topo.addr(peer)
+
+    g.dma_start(T.mine[:], T.x[:]).then_inc(T.sem.loaded, 16)
+    g.dma_start(T.y[:], T.x[:]).then_inc(T.sem.seeded, 16)
+
+    g.wait_ge(T.sem.loaded, 16)
+    g.remote_dma(T.land[:], T.mine[:], T.sem.arrived, T.sem.sent, pid, rid, ONE_ENGINE)
+
+    g.wait_ge(T.sem.seeded, 16)
+    g.wait_ge(T.sem.arrived, 1)
+    g.dma_start(T.y[:], T.land[:], accum_op=AluOpType.add).then_inc(T.sem.stored, 16)
+
+    g.wait_ge(T.sem.sent, 1)
+    g.wait_ge(T.sem.stored, 16)

@@ -1,8 +1,8 @@
 from concourse.mybir import AluOpType
 
 SCRATCH = {
-    "mine": ("sbuf", [128, 1], "bfloat16"),
-    "land": ("sbuf", [128, 1], "bfloat16"),
+    "mine": ("dram", [128, 1], "bfloat16"),
+    "land": ("dram", [128, 1], "bfloat16"),
 }
 SEMAPHORES = ["loaded", "seeded", "sent", "arrived", "stored"]
 
@@ -14,7 +14,7 @@ def rank_program(g, core, T, topo):
     if rank is None:
         return
     peer = T.cores[1 - rank]
-    rid, pid, _sengine = topo.addr(peer)
+    rid, pid = topo.addr(peer)[:2]
 
     g.dma_start(T.mine[:], T.x[:]).then_inc(T.sem.loaded, 16)
     g.dma_start(T.y[:], T.x[:]).then_inc(T.sem.seeded, 16)

from concourse.mybir import AluOpType

SCRATCH = {
    "mine": ("dram", [128, 1], "bfloat16"),
    "land": ("dram", [128, 1], "bfloat16"),
}
SEMAPHORES = ["loaded", "seeded", "sent", "arrived", "stored"]

ONE_ENGINE = 0x1


def rank_program(g, core, T, topo):
    rank = T.rank_of(core)
    if rank is None:
        return
    peer = T.cores[1 - rank]
    rid, pid = topo.addr(peer)[:2]

    g.dma_start(T.mine[:], T.x[:]).then_inc(T.sem.loaded, 16)
    g.dma_start(T.y[:], T.x[:]).then_inc(T.sem.seeded, 16)

    g.wait_ge(T.sem.loaded, 16)
    g.remote_dma(T.land[:], T.mine[:], T.sem.arrived, T.sem.sent, pid, rid, ONE_ENGINE)

    g.wait_ge(T.sem.seeded, 16)
    g.wait_ge(T.sem.arrived, 1)
    g.dma_start(T.y[:], T.land[:], accum_op=AluOpType.add).then_inc(T.sem.stored, 16)

    g.wait_ge(T.sem.sent, 1)
    g.wait_ge(T.sem.stored, 16)
